import numpy as np
import ml_dtypes


def mxq(x, axis, fmt="e4m3"):
    dtype, down = {"e4m3": (ml_dtypes.float8_e4m3fn, 7), "e5m2": (ml_dtypes.float8_e5m2, 14)}[fmt]
    v = np.moveaxis(np.asarray(x, np.float32).astype(ml_dtypes.bfloat16).astype(np.float64), axis, -1)
    blocks = v.reshape(v.shape[:-1] + (-1, 32))
    amax = np.abs(blocks).max(-1, keepdims=True)
    byte = np.maximum(np.where(amax > 0, np.frexp(amax)[1] - 1 + 127, 0) - down, 1)
    scale = np.exp2(byte - 127.0)
    codes = (blocks / scale).astype(np.float32).astype(dtype).astype(np.float64)
    return np.moveaxis((codes * scale).reshape(v.shape), -1, axis)


WIDE = False


def mx_kscale(k):
    if not WIDE:
        return np.ones(k)
    levels = np.array([10, -10, 5, -5, 0])
    if k % 512:
        return np.exp2(np.random.permutation(np.resize(levels, k // 32))).repeat(32)
    a = np.empty((k // 512, 16))
    for p in range(k // 512):
        a[p, :8] = np.random.permutation(np.resize(levels, 8))
        for g in range(8):
            far = levels[np.abs(levels - a[p, g]) >= 10]
            a[p, g + 8] = far[np.random.randint(len(far))]
    return np.exp2(a.ravel()).repeat(32)


def f64(x):
    return np.asarray(x).astype(np.float64)


def striped(idx):
    return np.tile(idx.reshape(-1, 16).T, (8, 1)).astype(np.uint16)


def unstriped(offs):
    return offs[:16].T.reshape(-1).astype(np.int64)


E2M1 = np.array([0.0, 0.5, 1.0, 1.5, 2.0, 3.0, 4.0, 6.0, -0.0, -0.5, -1.0, -1.5, -2.0, -3.0, -4.0, -6.0])


def pack_weight(w, fmt):
    k, n = w.shape
    w = f64(np.asarray(w, np.float32).astype(ml_dtypes.bfloat16)).reshape(k // 32, 32, n)
    amax = np.abs(w).max(1)
    if fmt == "e4m3":
        byte = np.frexp(amax)[1] - 1 + 127 - 7
    else:
        mant, ex = np.frexp(amax / 6.0)
        byte = np.where(mant > 0.5, ex, ex - 1) + 127
    byte = np.clip(np.where(amax > 0, byte, 1), 1, 254)
    scaled = (w * np.exp2(127.0 - byte)[:, None, :]).reshape(k, n).astype(np.float32)
    by_word = np.ascontiguousarray(scaled.reshape(k // 512, 128, 4, n).transpose(0, 1, 3, 2))
    if fmt == "e4m3":
        words = by_word.astype(ml_dtypes.float8_e4m3fn).view(np.uint8)
    else:
        c = by_word.astype(ml_dtypes.float4_e2m1fn).view(np.uint8) & 0xF
        words = (c[..., 0::2] | (c[..., 1::2] << 4)).reshape(k // 512, 128, 2 * n)
    return np.ascontiguousarray(words), np.ascontiguousarray(byte.astype(np.uint8).reshape(k // 512, 16, n))


def unpack_weight(words, scales, fmt):
    g, _, n = scales.shape
    words = np.ascontiguousarray(words).reshape(g, 128, n, -1)
    if fmt == "e4m3":
        vals = words.view(ml_dtypes.float8_e4m3fn).astype(np.float64)
    else:
        nib = np.empty((g, 128, n, 4), np.uint8)
        nib[..., 0::2] = words & 0xF
        nib[..., 1::2] = words >> 4
        vals = E2M1[nib]
    vals = vals * np.repeat(np.exp2(scales.astype(np.float64) - 127.0), 8, axis=1)[..., None]
    return vals.transpose(0, 1, 3, 2).reshape(g * 512, n)


def gelu(v):
    return 0.5 * v * (1.0 + np.tanh(np.sqrt(2.0 / np.pi) * (v + 0.044715 * v**3)))


K, N, H, T, S, T2, P = 1024, 512, 1536, 2048, 512, 1024, 512


def setup_inputs():
    n = np.random.standard_normal
    s, q, u = mx_kscale(K)[:, None], mx_kscale(N)[:, None], mx_kscale(H)[:, None]
    d = {}
    d["tab_words"], d["tab_scales"] = pack_weight(n((K, T)) * s, "e4m3")
    d["offs"] = striped(np.random.permutation(T)[:S])
    d["offs2"] = striped(np.random.permutation(T2)[:S])
    d["offs3"] = striped(np.random.permutation(T2)[:P])
    d["w1_words"], d["w1_scales"] = pack_weight(n((K, N)) / K**0.5 / s * q.T, "e2m1")
    d["w2"] = (1.4 * n((N, H)) / N**0.5 / q * u.T).astype(np.float32)
    d["w3"] = (n((K, H)) / K**0.5 / s * u.T).astype(np.float32)
    d["wgs"] = np.exp(0.3 * n((128, S))).astype(np.float32)
    d["page0"] = (n((H, T2)) * u).astype(np.float32)
    d["base"] = (n((H, P)) * u).astype(np.float32)
    d["lim"] = ((0.4 * n(H) - 0.3) * u[:, 0]).astype(np.float32)
    d["gain"] = (1.3 * n(H) / H**0.5 / u[:, 0]**2).astype(np.float32)
    d["slot"] = n(T2).astype(np.float32)
    return d


def reference(tab_words, tab_scales, offs, offs2, offs3, w1_words, w1_scales,
              w2, w3, wgs, page0, base, lim, gain, slot):
    v = unpack_weight(tab_words, tab_scales, "e4m3")[:, unstriped(offs)]
    w1 = unpack_weight(w1_words, w1_scales, "e2m1")
    mag = np.abs(w1.T @ v)
    deep = mxq(f64(w2), 0, "e4m3").T @ mxq(mag, 0, "e4m3")
    near = mxq(f64(w3), 0, "e4m3").T @ v
    h = np.maximum(deep, near)
    page = f64(page0).copy()
    page[:, unstriped(offs2)] = np.tile(f64(wgs), (H // 128, 1)) * h
    x = np.maximum(f64(base) - page[:, unstriped(offs3)], f64(lim)[:, None])
    x = x * f64(gain)[:, None]
    e = mxq(page, 0, "e4m3").T @ mxq(x, 0, "e4m3")
    return 1.0 / (1.0 + np.exp(-(e + f64(slot)[:, None])))

@@ -1,0 +1,372 @@
+from contextlib import ExitStack
+
+import concourse.mybir as mybir
+
+K, N, H, T, S, T2, PJ = 1024, 512, 1536, 2048, 512, 1024, 512
+FLOPS = 2 * (K * N * S + N * H * S + K * H * S + H * T2 * PJ)
+
+F32 = mybir.dt.float32
+BF16 = mybir.dt.bfloat16
+I32 = mybir.dt.int32
+U32 = mybir.dt.uint32
+U16 = mybir.dt.uint16
+U8 = mybir.dt.uint8
+FP8X4 = mybir.dt.float8_e4m3fn_x4
+FP4X4 = mybir.dt.float4_e2m1fn_x4
+ALU = mybir.AluOpType
+ACT = mybir.ActivationFunctionType
+
+P = 128
+PACK = 4
+KP = P * PACK
+BLOCKS = H // KP
+SLICES = BLOCKS * PACK
+CHUNKS = T2 // P
+
+
+def tile_list_silo_watch_page_kernel(
+    tc, tab_words, tab_scales, offs, offs2, offs3, w1_words, w1_scales,
+    w2, w3, wgs, page0, base, lim, gain, slot, out,
+):
+    nc = tc.nc
+    with ExitStack() as ctx:
+        keep = ctx.enter_context(tc.tile_pool(name="keep", bufs=1))
+        work = ctx.enter_context(tc.tile_pool(name="work", bufs=2))
+        psum = ctx.enter_context(tc.psum_pool(name="psum", bufs=8))
+
+        def big(shape, dtype, name):
+            return work.tile(shape, dtype, name=name, tag="big", bufs=5, align_bytes=64)
+
+        def bank(shape, name):
+            return psum.tile(shape, F32, name=name, tag="bank")
+
+        o1 = keep.tile([P, S // 16], U16, name="o1")
+        o2 = keep.tile([P, S // 16], U16, name="o2")
+        o3 = keep.tile([P, PJ // 16], U16, name="o3")
+        nc.sync.dma_start(o1[:], offs)
+
+        tabs = keep.tile([P, 2 * T], U8, name="tabs", align_bytes=64)
+        nc.vector.memset(tabs[:].bitcast(I32), 0)
+        w1s_raw = keep.tile([P, 2 * N], U8, name="w1s_raw", align_bytes=64)
+        nc.gpsimd.memset(w1s_raw[:].bitcast(I32), 0)
+        warm = keep.tile([P, 2], F32, name="warm")
+        nc.vector.memset(warm[:, 0:1], 0.0)
+
+        tabw = []
+        w1_raw = keep.tile([P, 2, 2 * N], U8, name="w1_raw", align_bytes=64)
+        nc.sync.dma_start(w1_raw[:].bitcast(I32), w1_words.rearrange("a p c -> p a c").bitcast(I32))
+        for q in range(4):
+            nc.sync.dma_start(
+                w1s_raw[32 * q : 32 * q + 4, :].bitcast(I32).rearrange("p (a c) -> p a c", a=2),
+                w1_scales[:, 4 * q : 4 * q + 4, :].rearrange("a r c -> r a c").bitcast(I32),
+            )
+        for a in range(2):
+            tw = big([P, T], I32, f"tabw{a}")
+            nc.sync.dma_start(tw[:], tab_words[a].rearrange("p n t -> p (n t)").bitcast(I32))
+            tabw.append(tw)
+            if a == 0:
+                for q in range(4):
+                    nc.sync.dma_start(
+                        tabs[32 * q : 32 * q + 4, :].bitcast(I32).rearrange("p (a c) -> p a c", a=2),
+                        tab_scales[:, 4 * q : 4 * q + 4, :].rearrange("a r c -> r a c").bitcast(I32),
+                    )
+        nc.scalar.activation(warm[:, 1:2], warm[:, 0:1], ACT.Sigmoid)
+
+        lim_sb = keep.tile([P, BLOCKS, PACK], F32, name="lim_sb")
+        gain_sb = keep.tile([P, BLOCKS, PACK], F32, name="gain_sb")
+        slot_sb = keep.tile([P, CHUNKS], F32, name="slot_sb")
+        neg_lim = keep.tile([P, SLICES], F32, name="neg_lim")
+        neg_gain = keep.tile([P, SLICES], F32, name="neg_gain")
+
+        w_raw = {}
+        pages, bases = {}, {}
+
+        def load_w(b, g):
+            src = w2 if g == 0 else w3[(g - 1) * KP : g * KP, :]
+            raw = big([P, PACK, KP], F32, f"w_raw{b}_{g}")
+            nc.sync.dma_start(raw[:], src[:, b * KP : (b + 1) * KP].rearrange("(p j) c -> p j c", j=PACK))
+            w_raw[b, g] = raw
+
+        def rows(src, s):
+            b, t = divmod(s, PACK)
+            return src[b * KP : (b + 1) * KP, :].rearrange("(p t) c -> p t c", t=PACK)[:, t, :]
+
+        def load_page(s):
+            pg = work.tile([P, T2], F32, name=f"page{s}", tag="page", bufs=7)
+            nc.sync.dma_start(pg[:], rows(page0, s))
+            pages[s] = pg
+
+        def load_base(s):
+            bs = work.tile([P, PJ], F32, name=f"base{s}", tag="base", bufs=7)
+            nc.sync.dma_start(bs[:], rows(base, s))
+            bases[s] = bs
+
+        wg = keep.tile([P, PACK, S], F32, name="wg")
+        wgs_rows = wgs.rearrange("(q t) j -> q t j", t=PACK)
+
+        def load_wg(t0, t1):
+            for q in range(4):
+                nc.sync.dma_start(wg[32 * q : 32 * q + 32, t0:t1, :], wgs_rows[:, t0:t1, :])
+
+        for g in (1, 2, 0):
+            load_w(0, g)
+        load_page(0)
+        load_wg(0, 1)
+        nc.sync.dma_start(o2[:], offs2)
+        load_page(1)
+        nc.sync.dma_start(o3[:], offs3)
+        load_base(0)
+        load_wg(1, PACK)
+        nc.sync.dma_start(lim_sb[:], lim.rearrange("(a p t) -> p a t", p=P, t=PACK))
+        nc.sync.dma_start(gain_sb[:], gain.rearrange("(a p t) -> p a t", p=P, t=PACK))
+
+        w1d = keep.tile([P, 2, 2 * N], U8, name="w1d", align_bytes=64)
+        nc.vector.tensor_copy(
+            w1d[:].rearrange("p a (t q e) -> p a q t e", t=PACK, e=2),
+            w1_raw[:].rearrange("p a (q t e) -> p a q t e", t=PACK, e=2),
+        )
+        w1s = keep.tile([P, 2, N], U8, name="w1s", align_bytes=64)
+        nc.vector.tensor_copy(
+            w1s[:].rearrange("p a (t q) -> p a q t", t=PACK),
+            w1s_raw[:].rearrange("p (a q t) -> p a q t", a=2, t=PACK),
+        )
+        vw, vs = [], []
+        for a in range(2):
+            words = keep.tile([P, S], U32, name=f"vw{a}", align_bytes=64)
+            scales = keep.tile([P, S], U8, name=f"vs{a}", align_bytes=64)
+            nc.vector.tensor_copy(words[:], tabw[a][:].bitcast(U32).indirect(o1[:]))
+            nc.vector.tensor_copy(scales[:], tabs[:, a * T : (a + 1) * T].indirect(o1[:]))
+            vw.append(words)
+            vs.append(scales)
+
+        mag_banks = [bank([P, PACK, P], f"mag_bank{c}") for c in range(4)]
+        for a in range(2):
+            for c in range(4):
+                cols = slice(c * P, (c + 1) * P)
+                for t in range(PACK):
+                    nc.tensor.matmul_mx(
+                        mag_banks[c][:, t, :],
+                        lhsT=w1d[:, a, 2 * P * t : 2 * P * (t + 1)].bitcast(FP4X4),
+                        lhsT_scale=w1s[:, a, P * t : P * (t + 1)],
+                        rhs=vw[a][:, cols].bitcast(FP8X4),
+                        rhs_scale=vs[a][:, cols],
+                        start=(a == 0 and t == 0),
+                        stop=(a == 1 and t == PACK - 1),
+                    )
+        mag16 = keep.tile([P, S, PACK], BF16, name="mag16", align_bytes=64)
+        for c in range(4):
+            nc.scalar.activation(
+                mag16[:, c * P : (c + 1) * P, :], mag_banks[c][:].rearrange("p t n -> p n t"), ACT.Abs
+            )
+        mag_q = keep.tile([P, S], U32, name="mag_q", align_bytes=64)
+        mag_s = keep.tile([P, S], U8, name="mag_s", align_bytes=64)
+
+        w16, w_q, w_s = {}, {}, {}
+
+        def cast_w(b, g, half, engine):
+            if (b, g) not in w16:
+                w16[b, g] = work.tile([P, PACK, P, PACK], BF16, name=f"w16_{b}_{g}", tag="w16", bufs=3, align_bytes=64)
+            ts = slice(2 * half, 2 * half + 2)
+            dst = w16[b, g][:, ts, :, :].rearrange("p t m j -> p m j t")
+            src = w_raw[b, g][:].rearrange("p j (m t) -> p m j t", t=PACK)[:, :, :, ts]
+            if engine == "vector":
+                nc.vector.tensor_copy(dst, src)
+            else:
+                nc.scalar.copy(dst, src)
+
+        def quant_w(b, g, t0, t1):
+            if (b, g) not in w_q:
+                w_q[b, g] = work.tile([P, KP], U32, name=f"w_q{b}_{g}", tag="w_q", bufs=6, align_bytes=64)
+                w_s[b, g] = work.tile([P, KP], U8, name=f"w_s{b}_{g}", tag="w_s", bufs=6, align_bytes=64)
+            cols = slice(t0 * P, t1 * P)
+            nc.vector.quantize_mx(
+                w_q[b, g][:, cols].bitcast(FP8X4), w_s[b, g][:, cols],
+                w16[b, g][:, t0:t1, :, :].rearrange("p t m j -> p (t m j)"),
+            )
+
+        cast_w(0, 1, 0, "vector")
+        cast_w(0, 1, 1, "vector")
+        quant_w(0, 1, 0, PACK)
+        nc.vector.quantize_mx(mag_q[:].bitcast(FP8X4), mag_s[:], mag16[:].rearrange("p n t -> p (n t)"))
+        for g in (2, 0):
+            cast_w(0, g, 0, "vector")
+            quant_w(0, g, 0, 2)
+            cast_w(0, g, 1, "scalar")
+
+        near_sb, deep_bank, hs, ds = {}, {}, {}, {}
+
+        def products(s):
+            b, t = divmod(s, PACK)
+            cols = slice(t * P, (t + 1) * P)
+            near = bank([P, S], f"near{s}")
+            for a in range(2):
+                nc.tensor.matmul_mx(
+                    near[:], lhsT=w_q[b, 1 + a][:, cols].bitcast(FP8X4), lhsT_scale=w_s[b, 1 + a][:, cols],
+                    rhs=vw[a][:].bitcast(FP8X4), rhs_scale=vs[a][:], start=(a == 0), stop=(a == 1),
+                )
+            nsb = work.tile([P, S], F32, name=f"near_sb{s}", tag="near_sb", bufs=3)
+            nc.scalar.copy(nsb[:], near[:])
+            deep = bank([P, S], f"deep{s}")
+            nc.tensor.matmul_mx(
+                deep[:], lhsT=w_q[b, 0][:, cols].bitcast(FP8X4), lhsT_scale=w_s[b, 0][:, cols],
+                rhs=mag_q[:].bitcast(FP8X4), rhs_scale=mag_s[:], start=True, stop=True,
+            )
+            near_sb[s], deep_bank[s] = nsb, deep
+
+        def larger(s):
+            h = work.tile([P, S], F32, name=f"h{s}", tag="h", bufs=2)
+            nc.vector.tensor_tensor(h[:], deep_bank[s][:], near_sb[s][:], ALU.max)
+            hs[s] = h
+
+        def scatter(s):
+            nc.vector.tensor_tensor(pages[s][:].indirect(o2[:]), hs[s][:], wg[:, s % PACK, :], ALU.mult)
+
+        def gather(s):
+            d = work.tile([P, PJ], F32, name=f"d{s}", tag="d", bufs=2)
+            nc.vector.tensor_tensor(d[:], pages[s][:].indirect(o3[:]), bases[s][:], ALU.subtract)
+            ds[s] = d
+
+        x_planes, x16, x_q, x_s = {}, {}, {}, {}
+        page_planes, page16, page_q, page_s = {}, {}, {}, {}
+
+        def clamp(s):
+            b, t = divmod(s, PACK)
+            if t == 0:
+                x_planes[b] = work.tile([P, PACK, PJ], BF16, name=f"x_planes{b}", tag="x_planes")
+            nc.vector.tensor_scalar(
+                x_planes[b][:, t, :], ds[s][:], neg_lim[:, s : s + 1], neg_gain[:, s : s + 1], ALU.min, ALU.mult
+            )
+
+        def weave(dst, src, engine):
+            dst = dst.rearrange("p (c i) t -> p c t i", i=4)
+            src = src.rearrange("p t (c i) -> p c t i", i=4)
+            if engine == "vector":
+                nc.vector.tensor_copy(dst, src)
+            else:
+                nc.scalar.copy(dst, src)
+
+        def weave_x(b):
+            x16[b] = work.tile([P, PJ, PACK], BF16, name=f"x16_{b}", tag="x16", bufs=1, align_bytes=64)
+            if b == BLOCKS - 1:
+                weave(x16[b][:], x_planes[b][:], "vector")
+            else:
+                for u in range(2):
+                    cols = slice(u * 256, (u + 1) * 256)
+                    weave(x16[b][:, cols, :], x_planes[b][:, :, cols], "scalar")
+
+        def quant_x(b):
+            x_q[b] = keep.tile([P, PJ], U32, name=f"x_q{b}", align_bytes=64)
+            x_s[b] = keep.tile([P, PJ], U8, name=f"x_s{b}", align_bytes=64)
+            nc.vector.quantize_mx(x_q[b][:].bitcast(FP8X4), x_s[b][:], x16[b][:].rearrange("p n t -> p (n t)"))
+
+        def cast_page(s):
+            b, t = divmod(s, PACK)
+            if t == 0:
+                page16[b] = work.tile([P, T2, PACK], BF16, name=f"page16_{b}", tag="page16", align_bytes=64)
+            if b == BLOCKS - 1:
+                for u in range(2):
+                    cols = slice(u * 512, (u + 1) * 512)
+                    nc.scalar.copy(page16[b][:, cols, t], pages[s][:, cols])
+            else:
+                if t == 0:
+                    page_planes[b] = work.tile([P, PACK, T2], BF16, name=f"page_planes{b}", tag="page_planes")
+                nc.scalar.copy(page_planes[b][:, t, :], pages[s][:])
+
+        def weave_page(b):
+            for u in range(4):
+                cols = slice(u * 256, (u + 1) * 256)
+                weave(page16[b][:, cols, :], page_planes[b][:, :, cols], "scalar")
+
+        def quant_page(b, u):
+            if u == 0:
+                page_q[b] = keep.tile([P, T2], U32, name=f"page_q{b}", align_bytes=64)
+                page_s[b] = keep.tile([P, T2], U8, name=f"page_s{b}", align_bytes=64)
+            cols = slice(u * 512, (u + 1) * 512)
+            nc.vector.quantize_mx(
+                page_q[b][:, cols].bitcast(FP8X4), page_s[b][:, cols],
+                page16[b][:, cols, :].rearrange("p m t -> p (m t)"),
+            )
+
+        e_banks = {}
+
+        def score(c, b):
+            if b == 0:
+                e_banks[c] = bank([P, PJ], f"e{c}")
+            cols = slice(c * P, (c + 1) * P)
+            nc.tensor.matmul_mx(
+                e_banks[c][:], lhsT=page_q[b][:, cols].bitcast(FP8X4), lhsT_scale=page_s[b][:, cols],
+                rhs=x_q[b][:].bitcast(FP8X4), rhs_scale=x_s[b][:], start=(b == 0), stop=(b == BLOCKS - 1),
+            )
+
+        products(0)
+        larger(0)
+        products(1)
+        larger(1)
+        for g in (2, 0):
+            quant_w(0, g, 2, PACK)
+
+        nc.scalar.mul(neg_lim[:], lim_sb[:].rearrange("p a t -> p (a t)"), -1.0)
+        nc.scalar.mul(neg_gain[:], gain_sb[:].rearrange("p a t -> p (a t)"), -1.0)
+
+        last = SLICES - 1
+        for s in range(SLICES):
+            b, t = divmod(s, PACK)
+            if b + 1 < BLOCKS:
+                if t == 0:
+                    load_w(b + 1, 1)
+                    load_w(b + 1, 2)
+                if t == 1:
+                    load_w(b + 1, 0)
+            if s + 2 == last:
+                load_base(s + 1)
+                load_page(s + 2)
+                load_base(s + 2)
+            elif s + 2 < last:
+                load_page(s + 2)
+                load_base(s + 1)
+            if s == PACK:
+                with nc.allow_non_contiguous_dma(reason="one bias value a partition"):
+                    nc.sync.dma_start(slot_sb[:], slot.rearrange("(c p) -> p c", p=P))
+            if b + 1 < BLOCKS and t < 2:
+                for g in ((1, 2) if t == 0 else (0,)):
+                    cast_w(b + 1, g, 0, "scalar")
+                    cast_w(b + 1, g, 1, "scalar")
+                    quant_w(b + 1, g, 0, PACK)
+            if s + 2 < SLICES:
+                products(s + 2)
+            if s == last:
+                gather(s - 1)
+            scatter(s)
+            cast_page(s)
+            if 0 < s < last:
+                gather(s - 1)
+            if s + 2 < SLICES:
+                larger(s + 2)
+            if s > 0:
+                clamp(s - 1)
+            if t == PACK - 1 and b < BLOCKS - 1:
+                weave_page(b)
+            if t == 0 and b > 0:
+                weave_x(b - 1)
+            if t == 1 and b > 0:
+                quant_page(b - 1, 0)
+                quant_page(b - 1, 1)
+                quant_x(b - 1)
+            if s == last - 1:
+                for c in range(CHUNKS):
+                    for bb in range(BLOCKS - 1):
+                        score(c, bb)
+        b = BLOCKS - 1
+        gather(last)
+        clamp(last)
+        weave_x(b)
+        quant_page(b, 0)
+        quant_x(b)
+        quant_page(b, 1)
+        for half in range(2):
+            res = big([P, 4, PJ], F32, f"res{half}")
+            for i in range(4):
+                c = 4 * half + i
+                score(c, b)
+                nc.scalar.activation(res[:, i, :], e_banks[c][:], ACT.Sigmoid, bias=slot_sb[:, c : c + 1])
+                nc.sync.dma_start(out[c * P : (c + 1) * P, :], res[:, i, :])

@@ -77,6 +77,7 @@ def tile_list_silo_watch_page_kernel(
         slot_sb = keep.tile([P, CHUNKS], F32, name="slot_sb")
         neg_lim = keep.tile([P, SLICES], F32, name="neg_lim")
         neg_gain = keep.tile([P, SLICES], F32, name="neg_gain")
+        floor = keep.tile([P, SLICES], F32, name="floor")
 
         w_raw = {}
         pages, bases = {}, {}
@@ -97,33 +98,30 @@ def tile_list_silo_watch_page_kernel(
             pages[s] = pg
 
         def load_base(s):
-            bs = work.tile([P, PJ], F32, name=f"base{s}", tag="base", bufs=7)
+            bs = work.tile([P, PJ], F32, name=f"base{s}", tag="base", bufs=4)
             nc.sync.dma_start(bs[:], rows(base, s))
             bases[s] = bs
 
-        wg = keep.tile([P, PACK, S], F32, name="wg")
+        wg = [work.tile([P, S], F32, name=f"wg{t}", tag=f"wg{t}", bufs=1) for t in range(PACK)]
         wgs_rows = wgs.rearrange("(q t) j -> q t j", t=PACK)
 
-        def load_wg(t0, t1):
+        def load_wg(t):
             for q in range(4):
-                nc.sync.dma_start(wg[32 * q : 32 * q + 32, t0:t1, :], wgs_rows[:, t0:t1, :])
+                nc.sync.dma_start(wg[t][32 * q : 32 * q + 32, :], wgs_rows[:, t, :])
 
         for g in (1, 2, 0):
             load_w(0, g)
         load_page(0)
-        load_wg(0, 1)
+        load_wg(0)
         nc.sync.dma_start(o2[:], offs2)
+        load_wg(1)
+        load_w(1, 1)
         load_page(1)
-        nc.sync.dma_start(o3[:], offs3)
-        load_base(0)
-        load_wg(1, PACK)
-        nc.sync.dma_start(lim_sb[:], lim.rearrange("(a p t) -> p a t", p=P, t=PACK))
-        nc.sync.dma_start(gain_sb[:], gain.rearrange("(a p t) -> p a t", p=P, t=PACK))
 
         w1d = keep.tile([P, 2, 2 * N], U8, name="w1d", align_bytes=64)
         nc.vector.tensor_copy(
-            w1d[:].rearrange("p a (t q e) -> p a q t e", t=PACK, e=2),
-            w1_raw[:].rearrange("p a (q t e) -> p a q t e", t=PACK, e=2),
+            w1d[:].bitcast(U16).rearrange("p a (t q) -> p a q t", t=PACK),
+            w1_raw[:].bitcast(U16).rearrange("p a (q t) -> p a q t", t=PACK),
         )
         w1s = keep.tile([P, 2, N], U8, name="w1s", align_bytes=64)
         nc.vector.tensor_copy(
@@ -153,45 +151,48 @@ def tile_list_silo_watch_page_kernel(
                         start=(a == 0 and t == 0),
                         stop=(a == 1 and t == PACK - 1),
                     )
-        mag16 = keep.tile([P, S, PACK], BF16, name="mag16", align_bytes=64)
+        mag16 = work.tile([P, S, PACK], BF16, name="mag16", tag="first0", bufs=1, align_bytes=64)
         for c in range(4):
             nc.scalar.activation(
                 mag16[:, c * P : (c + 1) * P, :], mag_banks[c][:].rearrange("p t n -> p n t"), ACT.Abs
             )
-        mag_q = keep.tile([P, S], U32, name="mag_q", align_bytes=64)
         mag_s = keep.tile([P, S], U8, name="mag_s", align_bytes=64)
 
-        w16, w_q, w_s = {}, {}, {}
+        w_q, w_s = {}, {}
 
-        def cast_w(b, g, half, engine):
-            if (b, g) not in w16:
-                w16[b, g] = work.tile([P, PACK, P, PACK], BF16, name=f"w16_{b}_{g}", tag="w16", bufs=3, align_bytes=64)
-            ts = slice(2 * half, 2 * half + 2)
-            dst = w16[b, g][:, ts, :, :].rearrange("p t m j -> p m j t")
-            src = w_raw[b, g][:].rearrange("p j (m t) -> p m j t", t=PACK)[:, :, :, ts]
+        def cast_w(b, g, half, stage, engine):
+            dst = stage.rearrange("p t m j -> p m j t")
+            src = w_raw[b, g][:].rearrange("p j (m t) -> p m j t", t=PACK)[:, :, :, 2 * half : 2 * half + 2]
             if engine == "vector":
                 nc.vector.tensor_copy(dst, src)
             else:
                 nc.scalar.copy(dst, src)
 
-        def quant_w(b, g, t0, t1):
-            if (b, g) not in w_q:
-                w_q[b, g] = work.tile([P, KP], U32, name=f"w_q{b}_{g}", tag="w_q", bufs=6, align_bytes=64)
+        def quant_w(b, g, t0, t1, stage, codes=None):
+            width = (t1 - t0) * P
+            if codes is None:
+                codes = work.tile([P, width], U32, name=f"w_q{b}_{g}", tag="w_q", bufs=6, align_bytes=64)[:]
+            if (b, g) not in w_s:
                 w_s[b, g] = work.tile([P, KP], U8, name=f"w_s{b}_{g}", tag="w_s", bufs=6, align_bytes=64)
-            cols = slice(t0 * P, t1 * P)
+            for t in range(t0, t1):
+                w_q[b, g, t] = codes[:, (t - t0) * P : (t - t0 + 1) * P]
             nc.vector.quantize_mx(
-                w_q[b, g][:, cols].bitcast(FP8X4), w_s[b, g][:, cols],
-                w16[b, g][:, t0:t1, :, :].rearrange("p t m j -> p (t m j)"),
+                codes.bitcast(FP8X4), w_s[b, g][:, t0 * P : t1 * P], stage.rearrange("p t m j -> p (t m j)")
             )
 
-        cast_w(0, 1, 0, "vector")
-        cast_w(0, 1, 1, "vector")
-        quant_w(0, 1, 0, PACK)
-        nc.vector.quantize_mx(mag_q[:].bitcast(FP8X4), mag_s[:], mag16[:].rearrange("p n t -> p (n t)"))
-        for g in (2, 0):
-            cast_w(0, g, 0, "vector")
-            quant_w(0, g, 0, 2)
-            cast_w(0, g, 1, "scalar")
+        def prepare_w(b, g):
+            stage = work.tile([P, PACK, P, PACK], BF16, name=f"w16_{b}_{g}", tag="w16", bufs=3, align_bytes=64)
+            for half in range(2):
+                cast_w(b, g, half, stage[:, 2 * half : 2 * half + 2], "scalar")
+            quant_w(b, g, 0, PACK, stage[:])
+
+        for g in (1, 2, 0):
+            stage = work.tile([P, 2, P, PACK], BF16, name=f"w16_first{g}", tag=f"first{g}", bufs=1, align_bytes=64)
+            cast_w(0, g, 0, stage[:], "vector")
+            quant_w(0, g, 0, 2, stage[:])
+            if g == 2:
+                mag_q = work.tile([P, S], U32, name="mag_q", tag="first2", bufs=1, align_bytes=64)
+                nc.vector.quantize_mx(mag_q[:].bitcast(FP8X4), mag_s[:], mag16[:].rearrange("p n t -> p (n t)"))
 
         near_sb, deep_bank, hs, ds = {}, {}, {}, {}
 
@@ -201,40 +202,53 @@ def tile_list_silo_watch_page_kernel(
             near = bank([P, S], f"near{s}")
             for a in range(2):
                 nc.tensor.matmul_mx(
-                    near[:], lhsT=w_q[b, 1 + a][:, cols].bitcast(FP8X4), lhsT_scale=w_s[b, 1 + a][:, cols],
+                    near[:], lhsT=w_q[b, 1 + a, t].bitcast(FP8X4), lhsT_scale=w_s[b, 1 + a][:, cols],
                     rhs=vw[a][:].bitcast(FP8X4), rhs_scale=vs[a][:], start=(a == 0), stop=(a == 1),
                 )
             nsb = work.tile([P, S], F32, name=f"near_sb{s}", tag="near_sb", bufs=3)
             nc.scalar.copy(nsb[:], near[:])
             deep = bank([P, S], f"deep{s}")
             nc.tensor.matmul_mx(
-                deep[:], lhsT=w_q[b, 0][:, cols].bitcast(FP8X4), lhsT_scale=w_s[b, 0][:, cols],
+                deep[:], lhsT=w_q[b, 0, t].bitcast(FP8X4), lhsT_scale=w_s[b, 0][:, cols],
                 rhs=mag_q[:].bitcast(FP8X4), rhs_scale=mag_s[:], start=True, stop=True,
             )
             near_sb[s], deep_bank[s] = nsb, deep
 
         def larger(s):
-            h = work.tile([P, S], F32, name=f"h{s}", tag="h", bufs=2)
+            tag = "h_a" if s % 2 == 0 and s != 2 else "h_b"
+            h = work.tile([P, S], F32, name=f"h{s}", tag=tag, bufs=1, align_bytes=64)
             nc.vector.tensor_tensor(h[:], deep_bank[s][:], near_sb[s][:], ALU.max)
             hs[s] = h
 
         def scatter(s):
-            nc.vector.tensor_tensor(pages[s][:].indirect(o2[:]), hs[s][:], wg[:, s % PACK, :], ALU.mult)
+            nc.vector.tensor_tensor(pages[s][:].indirect(o2[:]), hs[s][:], wg[s % PACK][:], ALU.mult)
 
-        def gather(s):
-            d = work.tile([P, PJ], F32, name=f"d{s}", tag="d", bufs=2)
-            nc.vector.tensor_tensor(d[:], pages[s][:].indirect(o3[:]), bases[s][:], ALU.subtract)
-            ds[s] = d
+        def gather(s, cols, minuend, dst):
+            entries = o3[:, cols.start // 16 : cols.stop // 16]
+            nc.vector.tensor_tensor(dst, pages[s][:].indirect(entries), minuend, ALU.subtract)
+            ds[s] = dst
 
         x_planes, x16, x_q, x_s = {}, {}, {}, {}
         page_planes, page16, page_q, page_s = {}, {}, {}, {}
 
-        def clamp(s):
+        def clamp(s, cols):
             b, t = divmod(s, PACK)
             if t == 0:
                 x_planes[b] = work.tile([P, PACK, PJ], BF16, name=f"x_planes{b}", tag="x_planes")
             nc.vector.tensor_scalar(
-                x_planes[b][:, t, :], ds[s][:], neg_lim[:, s : s + 1], neg_gain[:, s : s + 1], ALU.min, ALU.mult
+                x_planes[b][:, t, cols], ds[s], neg_lim[:, s : s + 1], neg_gain[:, s : s + 1],
+                ALU.min, ALU.mult,
+            )
+
+        def clamp_on_scalar(s):
+            b, t = divmod(s, PACK)
+            if t == 0:
+                x_planes[b] = work.tile([P, PACK, PJ], BF16, name=f"x_planes{b}", tag="x_planes")
+            above = work.tile([P, PJ], F32, name=f"above{s}", tag="above")
+            nc.scalar.activation(above[:], ds[s], ACT.Relu, bias=neg_lim[:, s : s + 1], scale=-1.0)
+            nc.scalar.activation(
+                x_planes[b][:, t, :], above[:], ACT.Identity,
+                bias=floor[:, s : s + 1], scale=gain_sb[:, b, t : t + 1],
             )
 
         def weave(dst, src, engine):
@@ -245,37 +259,31 @@ def tile_list_silo_watch_page_kernel(
             else:
                 nc.scalar.copy(dst, src)
 
-        def weave_x(b):
-            x16[b] = work.tile([P, PJ, PACK], BF16, name=f"x16_{b}", tag="x16", bufs=1, align_bytes=64)
-            if b == BLOCKS - 1:
-                weave(x16[b][:], x_planes[b][:], "vector")
-            else:
-                for u in range(2):
-                    cols = slice(u * 256, (u + 1) * 256)
-                    weave(x16[b][:, cols, :], x_planes[b][:, :, cols], "scalar")
+        def weave_x(b, cols, engine):
+            if cols.start == 0:
+                x16[b] = work.tile([P, PJ, PACK], BF16, name=f"x16_{b}", tag="x16", bufs=1, align_bytes=64)
+            weave(x16[b][:, cols, :], x_planes[b][:, :, cols], engine)
 
-        def quant_x(b):
-            x_q[b] = keep.tile([P, PJ], U32, name=f"x_q{b}", align_bytes=64)
-            x_s[b] = keep.tile([P, PJ], U8, name=f"x_s{b}", align_bytes=64)
-            nc.vector.quantize_mx(x_q[b][:].bitcast(FP8X4), x_s[b][:], x16[b][:].rearrange("p n t -> p (n t)"))
+        def quant_x(b, cols):
+            if cols.start == 0:
+                x_q[b] = keep.tile([P, PJ], U32, name=f"x_q{b}", align_bytes=64)
+                x_s[b] = keep.tile([P, PJ], U8, name=f"x_s{b}", align_bytes=64)
+            nc.vector.quantize_mx(
+                x_q[b][:, cols].bitcast(FP8X4), x_s[b][:, cols], x16[b][:, cols, :].rearrange("p n t -> p (n t)")
+            )
 
         def cast_page(s):
             b, t = divmod(s, PACK)
             if t == 0:
-                page16[b] = work.tile([P, T2, PACK], BF16, name=f"page16_{b}", tag="page16", align_bytes=64)
-            if b == BLOCKS - 1:
-                for u in range(2):
-                    cols = slice(u * 512, (u + 1) * 512)
-                    nc.scalar.copy(page16[b][:, cols, t], pages[s][:, cols])
-            else:
-                if t == 0:
-                    page_planes[b] = work.tile([P, PACK, T2], BF16, name=f"page_planes{b}", tag="page_planes")
-                nc.scalar.copy(page_planes[b][:, t, :], pages[s][:])
+                page_planes[b] = work.tile([P, PACK, T2], BF16, name=f"page_planes{b}", tag="page_planes")
+            nc.scalar.copy(page_planes[b][:, t, :], pages[s][:])
 
         def weave_page(b):
-            for u in range(4):
-                cols = slice(u * 256, (u + 1) * 256)
-                weave(page16[b][:, cols, :], page_planes[b][:, :, cols], "scalar")
+            for u in range(2):
+                page16[b, u] = work.tile([P, T2 // 2, PACK], BF16, name=f"page16_{b}_{u}", tag=f"page16_{u}", bufs=1, align_bytes=64)
+                for v in range(2):
+                    lo = u * 512 + v * 256
+                    weave(page16[b, u][:, v * 256 : (v + 1) * 256, :], page_planes[b][:, :, lo : lo + 256], "scalar")
 
         def quant_page(b, u):
             if u == 0:
@@ -283,90 +291,137 @@ def tile_list_silo_watch_page_kernel(
                 page_s[b] = keep.tile([P, T2], U8, name=f"page_s{b}", align_bytes=64)
             cols = slice(u * 512, (u + 1) * 512)
             nc.vector.quantize_mx(
-                page_q[b][:, cols].bitcast(FP8X4), page_s[b][:, cols],
-                page16[b][:, cols, :].rearrange("p m t -> p (m t)"),
+                page_q[b][:, cols].bitcast(FP8X4), page_s[b][:, cols], page16[b, u][:].rearrange("p m t -> p (m t)")
             )
 
+        halves = (slice(0, PJ // 2), slice(PJ // 2, PJ))
+        whole = slice(0, PJ)
         e_banks = {}
 
-        def score(c, b):
+        def score(half, k, b):
             if b == 0:
-                e_banks[c] = bank([P, PJ], f"e{c}")
-            cols = slice(c * P, (c + 1) * P)
-            nc.tensor.matmul_mx(
-                e_banks[c][:], lhsT=page_q[b][:, cols].bitcast(FP8X4), lhsT_scale=page_s[b][:, cols],
-                rhs=x_q[b][:].bitcast(FP8X4), rhs_scale=x_s[b][:], start=(b == 0), stop=(b == BLOCKS - 1),
-            )
+                e_banks[half, k] = bank([P, 2, PJ // 2], f"e{half}_{k}")
+            for i in range(2):
+                cols = slice((2 * k + i) * P, (2 * k + i + 1) * P)
+                nc.tensor.matmul_mx(
+                    e_banks[half, k][:, i, :], lhsT=page_q[b][:, cols].bitcast(FP8X4), lhsT_scale=page_s[b][:, cols],
+                    rhs=x_q[b][:, halves[half]].bitcast(FP8X4), rhs_scale=x_s[b][:, halves[half]],
+                    start=(b == 0 and i == 0), stop=(b == BLOCKS - 1 and i == 1),
+                )
 
         products(0)
         larger(0)
         products(1)
         larger(1)
-        for g in (2, 0):
-            quant_w(0, g, 2, PACK)
-
-        nc.scalar.mul(neg_lim[:], lim_sb[:].rearrange("p a t -> p (a t)"), -1.0)
-        nc.scalar.mul(neg_gain[:], gain_sb[:].rearrange("p a t -> p (a t)"), -1.0)
+        scatter(0)
+        late = work.tile([P, 3, 2, P, PACK], BF16, name="w16_second", tag="first0", bufs=1, align_bytes=64)
+        late_q = work.tile([P, 3, 2 * P], U32, name="w_q_second", tag="h_a", bufs=1, align_bytes=64)
+        for g in (1, 2, 0):
+            cast_w(0, g, 1, late[:, g], "scalar")
+            quant_w(0, g, 2, PACK, late[:, g], late_q[:, g, :])
 
         last = SLICES - 1
+        later_w = [(b, g) for b in range(1, BLOCKS) for g in (1, 2, 0)]
+        wpos = [1, 2, 3, 4, 5, 6]
         for s in range(SLICES):
             b, t = divmod(s, PACK)
-            if b + 1 < BLOCKS:
-                if t == 0:
-                    load_w(b + 1, 1)
-                    load_w(b + 1, 2)
-                if t == 1:
-                    load_w(b + 1, 0)
-            if s + 2 == last:
-                load_base(s + 1)
-                load_page(s + 2)
-                load_base(s + 2)
-            elif s + 2 < last:
-                load_page(s + 2)
-                load_base(s + 1)
-            if s == PACK:
+            nxt = s + 2
+            if nxt < SLICES:
+                if nxt < PACK:
+                    load_wg(nxt)
+                for i in range(1, 6):
+                    if wpos[i] == nxt:
+                        load_w(*later_w[i])
+                load_page(nxt)
+                if s == 0:
+                    nc.sync.dma_start(lim_sb[:], lim.rearrange("(a p t) -> p a t", p=P, t=PACK))
+                    nc.sync.dma_start(gain_sb[:], gain.rearrange("(a p t) -> p a t", p=P, t=PACK))
+                    nc.sync.dma_start(o3[:], offs3)
+                    nc.scalar.mul(neg_lim[:], lim_sb[:].rearrange("p a t -> p (a t)"), -1.0)
+                    nc.scalar.mul(neg_gain[:], gain_sb[:].rearrange("p a t -> p (a t)"), -1.0)
+                    nc.vector.tensor_tensor(floor[:], neg_lim[:], neg_gain[:], ALU.mult)
+                if nxt < last:
+                    load_base(s)
+            if s == PACK + 2:
                 with nc.allow_non_contiguous_dma(reason="one bias value a partition"):
                     nc.sync.dma_start(slot_sb[:], slot.rearrange("(c p) -> p c", p=P))
-            if b + 1 < BLOCKS and t < 2:
-                for g in ((1, 2) if t == 0 else (0,)):
-                    cast_w(b + 1, g, 0, "scalar")
-                    cast_w(b + 1, g, 1, "scalar")
-                    quant_w(b + 1, g, 0, PACK)
-            if s + 2 < SLICES:
-                products(s + 2)
-            if s == last:
-                gather(s - 1)
-            scatter(s)
-            cast_page(s)
-            if 0 < s < last:
-                gather(s - 1)
-            if s + 2 < SLICES:
-                larger(s + 2)
             if s > 0:
-                clamp(s - 1)
-            if t == PACK - 1 and b < BLOCKS - 1:
-                weave_page(b)
-            if t == 0 and b > 0:
-                weave_x(b - 1)
+                scatter(s)
+            if s == last - 1:
+                tail_base = []
+                for half in range(2):
+                    bs = work.tile([P, 3, PJ // 2], F32, name=f"tail_base{half}", tag=f"wg{2 + half}", bufs=1)
+                    src = base[(BLOCKS - 1) * KP :, halves[half]].rearrange("(p t) c -> p t c", t=PACK)
+                    nc.sync.dma_start(bs[:], src[:, 1:PACK, :])
+                    tail_base.append(bs)
+            for i in range(6):
+                if max(wpos[i] - 1, 0) == s:
+                    prepare_w(*later_w[i])
+                    if 0 and i % 3 == 2:
+                        for r in range(4):
+                            products(4 * later_w[i][0] + r)
+            ready = [s + 1] if s < PACK else []
+            if PACK - 1 <= s and nxt < SLICES:
+                ready.append(nxt)
+            if s == 0:
+                ready = []
+            for r in ready:
+                if r not in near_sb:
+                    products(r)
+            cast_page(s)
+            if 2 <= s < last:
+                d = work.tile([P, PJ], F32, name=f"d{s - 2}", tag="d", bufs=2)
+                gather(s - 2, whole, bases[s - 2][:], d[:])
+            for r in ready:
+                larger(r)
+            if 2 <= s < last:
+                if s - 2 < 9 and s - 2 >= 0:
+                    clamp_on_scalar(s - 2)
+                else:
+                    clamp(s - 2, whole)
             if t == 1 and b > 0:
+                weave_page(b - 1)
+            if t == 2 and b > 0:
                 quant_page(b - 1, 0)
                 quant_page(b - 1, 1)
-                quant_x(b - 1)
+                for half in range(2):
+                    weave_x(b - 1, halves[half], "scalar")
+                quant_x(b - 1, whole)
             if s == last - 1:
-                for c in range(CHUNKS):
-                    for bb in range(BLOCKS - 1):
-                        score(c, bb)
+                for half in range(2):
+                    for k in range(CHUNKS // 2):
+                        for bb in range(BLOCKS - 1):
+                            score(half, k, bb)
+        weave_page(BLOCKS - 1)
         b = BLOCKS - 1
-        gather(last)
-        clamp(last)
-        weave_x(b)
-        quant_page(b, 0)
-        quant_x(b)
-        quant_page(b, 1)
         for half in range(2):
-            res = big([P, 4, PJ], F32, f"res{half}")
-            for i in range(4):
-                c = 4 * half + i
-                score(c, b)
-                nc.scalar.activation(res[:, i, :], e_banks[c][:], ACT.Sigmoid, bias=slot_sb[:, c : c + 1])
-                nc.sync.dma_start(out[c * P : (c + 1) * P, :], res[:, i, :])
+            cols = halves[half]
+            if half == 0:
+                d = work.tile([P, 3, PJ // 2], F32, name="d_tail0", tag="d", bufs=2)
+                dsts = [d[:, i, :] for i in range(3)]
+            else:
+                d = work.tile([P, PJ // 2], F32, name="d_tail1", tag="page16_0", bufs=1, align_bytes=64)
+                d_last = work.tile([P, 2, PJ // 2], F32, name="d_tail2", tag="page16_1", bufs=1, align_bytes=64)
+                dsts = [d[:], d_last[:, 0, :], d_last[:, 1, :]]
+            for i, s in enumerate(range(last - 2, SLICES)):
+                gather(s, cols, tail_base[half][:, i, :], dsts[i])
+            for s in range(last - 2, SLICES):
+                clamp(s, cols)
+            weave_x(b, cols, "vector")
+            if half == 0:
+                quant_page(b, 0)
+            quant_x(b, cols)
+            if half == 0:
+                quant_page(b, 1)
+            res = big([P, CHUNKS, PJ // 2], F32, f"res{half}")
+            for k in range(CHUNKS // 2):
+                score(half, k, b)
+                for i in range(2):
+                    c = 2 * k + i
+                    nc.scalar.activation(
+                        res[:, c, :], e_banks[half, k][:, i, :], ACT.Sigmoid, bias=slot_sb[:, c : c + 1]
+                    )
+                nc.sync.dma_start(
+                    out[2 * k * P : (2 * k + 2) * P, cols].rearrange("(i p) j -> p i j", p=P),
+                    res[:, 2 * k : 2 * k + 2, :],
+                )

@@ -49,8 +49,6 @@ def tile_list_silo_watch_page_kernel(
         nc.vector.memset(tabs[:].bitcast(I32), 0)
         w1s_raw = keep.tile([P, 2 * N], U8, name="w1s_raw", align_bytes=64)
         nc.gpsimd.memset(w1s_raw[:].bitcast(I32), 0)
-        warm = keep.tile([P, 2], F32, name="warm")
-        nc.vector.memset(warm[:, 0:1], 0.0)
 
         tabw = []
         w1_raw = keep.tile([P, 2, 2 * N], U8, name="w1_raw", align_bytes=64)
@@ -70,7 +68,6 @@ def tile_list_silo_watch_page_kernel(
                         tabs[32 * q : 32 * q + 4, :].bitcast(I32).rearrange("p (a c) -> p a c", a=2),
                         tab_scales[:, 4 * q : 4 * q + 4, :].rearrange("a r c -> r a c").bitcast(I32),
                     )
-        nc.scalar.activation(warm[:, 1:2], warm[:, 0:1], ACT.Sigmoid)
 
         lim_sb = keep.tile([P, BLOCKS, PACK], F32, name="lim_sb")
         gain_sb = keep.tile([P, BLOCKS, PACK], F32, name="gain_sb")
@@ -205,7 +202,7 @@ def tile_list_silo_watch_page_kernel(
                     near[:], lhsT=w_q[b, 1 + a, t].bitcast(FP8X4), lhsT_scale=w_s[b, 1 + a][:, cols],
                     rhs=vw[a][:].bitcast(FP8X4), rhs_scale=vs[a][:], start=(a == 0), stop=(a == 1),
                 )
-            nsb = work.tile([P, S], F32, name=f"near_sb{s}", tag="near_sb", bufs=3)
+            nsb = work.tile([P, S], F32, name=f"near_sb{s}", tag="near_sb", bufs=2)
             nc.scalar.copy(nsb[:], near[:])
             deep = bank([P, S], f"deep{s}")
             nc.tensor.matmul_mx(
@@ -261,7 +258,7 @@ def tile_list_silo_watch_page_kernel(
 
         def weave_x(b, cols, engine):
             if cols.start == 0:
-                x16[b] = work.tile([P, PJ, PACK], BF16, name=f"x16_{b}", tag="x16", bufs=1, align_bytes=64)
+                x16[b] = work.tile([P, PJ, PACK], BF16, name=f"x16_{b}", tag="x16", bufs=2, align_bytes=64)
             weave(x16[b][:, cols, :], x_planes[b][:, :, cols], engine)
 
         def quant_x(b, cols):
@@ -280,7 +277,7 @@ def tile_list_silo_watch_page_kernel(
 
         def weave_page(b):
             for u in range(2):
-                page16[b, u] = work.tile([P, T2 // 2, PACK], BF16, name=f"page16_{b}_{u}", tag=f"page16_{u}", bufs=1, align_bytes=64)
+                page16[b, u] = work.tile([P, T2 // 2, PACK], BF16, name=f"page16_{b}_{u}", tag=(f"page16_{u}" if b == 2 or 1 == 0 else f"page16x_{u}"), bufs=1, align_bytes=64)
                 for v in range(2):
                     lo = u * 512 + v * 256
                     weave(page16[b, u][:, v * 256 : (v + 1) * 256, :], page_planes[b][:, :, lo : lo + 256], "scalar")
@@ -310,15 +307,23 @@ def tile_list_silo_watch_page_kernel(
                 )
 
         products(0)
-        larger(0)
-        products(1)
-        larger(1)
-        scatter(0)
+        first_h = []
+        for half, tag in enumerate(("h_a", "h_b")):
+            h = work.tile([P, S // 2], F32, name=f"h0_{half}", tag=tag, bufs=1, align_bytes=64)
+            nc.vector.tensor_tensor(h[:], deep_bank[0][:, halves[half]], near_sb[0][:, halves[half]], ALU.max)
+            first_h.append(h)
+        for half in range(2):
+            cols = halves[half]
+            places = o2[:, cols.start // 16 : cols.stop // 16]
+            nc.vector.tensor_tensor(pages[0][:].indirect(places), first_h[half][:], wg[0][:, cols], ALU.mult)
         late = work.tile([P, 3, 2, P, PACK], BF16, name="w16_second", tag="first0", bufs=1, align_bytes=64)
         late_q = work.tile([P, 3, 2 * P], U32, name="w_q_second", tag="h_a", bufs=1, align_bytes=64)
         for g in (1, 2, 0):
             cast_w(0, g, 1, late[:, g], "scalar")
             quant_w(0, g, 2, PACK, late[:, g], late_q[:, g, :])
+            if g == 1:
+                products(1)
+                larger(1)
 
         last = SLICES - 1
         later_w = [(b, g) for b in range(1, BLOCKS) for g in (1, 2, 0)]
@@ -400,9 +405,15 @@ def tile_list_silo_watch_page_kernel(
                 d = work.tile([P, 3, PJ // 2], F32, name="d_tail0", tag="d", bufs=2)
                 dsts = [d[:, i, :] for i in range(3)]
             else:
-                d = work.tile([P, PJ // 2], F32, name="d_tail1", tag="page16_0", bufs=1, align_bytes=64)
-                d_last = work.tile([P, 2, PJ // 2], F32, name="d_tail2", tag="page16_1", bufs=1, align_bytes=64)
-                dsts = [d[:], d_last[:, 0, :], d_last[:, 1, :]]
+                if 0 == 0:
+                    d = work.tile([P, PJ // 2], F32, name="d_tail1", tag="page16_0", bufs=1, align_bytes=64)
+                    d_last = work.tile([P, 2, PJ // 2], F32, name="d_tail2", tag="page16_1", bufs=1, align_bytes=64)
+                    dsts = [d[:], d_last[:, 0, :], d_last[:, 1, :]]
+                else:
+                    d0 = work.tile([P, PJ // 2], F32, name="d_tail1a", tag="d_free", bufs=1)
+                    d = work.tile([P, PJ // 2], F32, name="d_tail1", tag="page16_0", bufs=1, align_bytes=64)
+                    d_last = work.tile([P, PJ // 2], F32, name="d_tail2", tag="page16_1", bufs=1, align_bytes=64)
+                    dsts = [d0[:], d[:], d_last[:]]
             for i, s in enumerate(range(last - 2, SLICES)):
                 gather(s, cols, tail_base[half][:, i, :], dsts[i])
             for s in range(last - 2, SLICES):

from contextlib import ExitStack

import concourse.mybir as mybir

K, N, H, T, S, T2, PJ = 1024, 512, 1536, 2048, 512, 1024, 512
FLOPS = 2 * (K * N * S + N * H * S + K * H * S + H * T2 * PJ)

F32 = mybir.dt.float32
BF16 = mybir.dt.bfloat16
I32 = mybir.dt.int32
U32 = mybir.dt.uint32
U16 = mybir.dt.uint16
U8 = mybir.dt.uint8
FP8X4 = mybir.dt.float8_e4m3fn_x4
FP4X4 = mybir.dt.float4_e2m1fn_x4
ALU = mybir.AluOpType
ACT = mybir.ActivationFunctionType

P = 128
PACK = 4
KP = P * PACK
BLOCKS = H // KP
SLICES = BLOCKS * PACK
CHUNKS = T2 // P


def tile_list_silo_watch_page_kernel(
    tc, tab_words, tab_scales, offs, offs2, offs3, w1_words, w1_scales,
    w2, w3, wgs, page0, base, lim, gain, slot, out,
):
    nc = tc.nc
    with ExitStack() as ctx:
        keep = ctx.enter_context(tc.tile_pool(name="keep", bufs=1))
        work = ctx.enter_context(tc.tile_pool(name="work", bufs=2))
        psum = ctx.enter_context(tc.psum_pool(name="psum", bufs=8))

        def big(shape, dtype, name):
            return work.tile(shape, dtype, name=name, tag="big", bufs=5, align_bytes=64)

        def bank(shape, name):
            return psum.tile(shape, F32, name=name, tag="bank")

        o1 = keep.tile([P, S // 16], U16, name="o1")
        o2 = keep.tile([P, S // 16], U16, name="o2")
        o3 = keep.tile([P, PJ // 16], U16, name="o3")
        nc.sync.dma_start(o1[:], offs)

        tabs = keep.tile([P, 2 * T], U8, name="tabs", align_bytes=64)
        nc.vector.memset(tabs[:].bitcast(I32), 0)
        w1s_raw = keep.tile([P, 2 * N], U8, name="w1s_raw", align_bytes=64)
        nc.gpsimd.memset(w1s_raw[:].bitcast(I32), 0)

        tabw = []
        w1_raw = keep.tile([P, 2, 2 * N], U8, name="w1_raw", align_bytes=64)
        nc.sync.dma_start(w1_raw[:].bitcast(I32), w1_words.rearrange("a p c -> p a c").bitcast(I32))
        for q in range(4):
            nc.sync.dma_start(
                w1s_raw[32 * q : 32 * q + 4, :].bitcast(I32).rearrange("p (a c) -> p a c", a=2),
                w1_scales[:, 4 * q : 4 * q + 4, :].rearrange("a r c -> r a c").bitcast(I32),
            )
        for a in range(2):
            tw = big([P, T], I32, f"tabw{a}")
            nc.sync.dma_start(tw[:], tab_words[a].rearrange("p n t -> p (n t)").bitcast(I32))
            tabw.append(tw)
            if a == 0:
                for q in range(4):
                    nc.sync.dma_start(
                        tabs[32 * q : 32 * q + 4, :].bitcast(I32).rearrange("p (a c) -> p a c", a=2),
                        tab_scales[:, 4 * q : 4 * q + 4, :].rearrange("a r c -> r a c").bitcast(I32),
                    )

        lim_sb = keep.tile([P, BLOCKS, PACK], F32, name="lim_sb")
        gain_sb = keep.tile([P, BLOCKS, PACK], F32, name="gain_sb")
        slot_sb = keep.tile([P, CHUNKS], F32, name="slot_sb")
        neg_lim = keep.tile([P, SLICES], F32, name="neg_lim")
        neg_gain = keep.tile([P, SLICES], F32, name="neg_gain")
        floor = keep.tile([P, SLICES], F32, name="floor")

        w_raw = {}
        pages, bases = {}, {}

        def load_w(b, g):
            src = w2 if g == 0 else w3[(g - 1) * KP : g * KP, :]
            raw = big([P, PACK, KP], F32, f"w_raw{b}_{g}")
            nc.sync.dma_start(raw[:], src[:, b * KP : (b + 1) * KP].rearrange("(p j) c -> p j c", j=PACK))
            w_raw[b, g] = raw

        def rows(src, s):
            b, t = divmod(s, PACK)
            return src[b * KP : (b + 1) * KP, :].rearrange("(p t) c -> p t c", t=PACK)[:, t, :]

        def load_page(s):
            pg = work.tile([P, T2], F32, name=f"page{s}", tag="page", bufs=7)
            nc.sync.dma_start(pg[:], rows(page0, s))
            pages[s] = pg

        def load_base(s):
            bs = work.tile([P, PJ], F32, name=f"base{s}", tag="base", bufs=4)
            nc.sync.dma_start(bs[:], rows(base, s))
            bases[s] = bs

        wg = [work.tile([P, S], F32, name=f"wg{t}", tag=f"wg{t}", bufs=1) for t in range(PACK)]
        wgs_rows = wgs.rearrange("(q t) j -> q t j", t=PACK)

        def load_wg(t):
            for q in range(4):
                nc.sync.dma_start(wg[t][32 * q : 32 * q + 32, :], wgs_rows[:, t, :])

        for g in (1, 2, 0):
            load_w(0, g)
        load_page(0)
        load_wg(0)
        nc.sync.dma_start(o2[:], offs2)
        load_wg(1)
        load_w(1, 1)
        load_page(1)

        w1d = keep.tile([P, 2, 2 * N], U8, name="w1d", align_bytes=64)
        nc.vector.tensor_copy(
            w1d[:].bitcast(U16).rearrange("p a (t q) -> p a q t", t=PACK),
            w1_raw[:].bitcast(U16).rearrange("p a (q t) -> p a q t", t=PACK),
        )
        w1s = keep.tile([P, 2, N], U8, name="w1s", align_bytes=64)
        nc.vector.tensor_copy(
            w1s[:].rearrange("p a (t q) -> p a q t", t=PACK),
            w1s_raw[:].rearrange("p (a q t) -> p a q t", a=2, t=PACK),
        )
        vw, vs = [], []
        for a in range(2):
            words = keep.tile([P, S], U32, name=f"vw{a}", align_bytes=64)
            scales = keep.tile([P, S], U8, name=f"vs{a}", align_bytes=64)
            nc.vector.tensor_copy(words[:], tabw[a][:].bitcast(U32).indirect(o1[:]))
            nc.vector.tensor_copy(scales[:], tabs[:, a * T : (a + 1) * T].indirect(o1[:]))
            vw.append(words)
            vs.append(scales)

        mag_banks = [bank([P, PACK, P], f"mag_bank{c}") for c in range(4)]
        for a in range(2):
            for c in range(4):
                cols = slice(c * P, (c + 1) * P)
                for t in range(PACK):
                    nc.tensor.matmul_mx(
                        mag_banks[c][:, t, :],
                        lhsT=w1d[:, a, 2 * P * t : 2 * P * (t + 1)].bitcast(FP4X4),
                        lhsT_scale=w1s[:, a, P * t : P * (t + 1)],
                        rhs=vw[a][:, cols].bitcast(FP8X4),
                        rhs_scale=vs[a][:, cols],
                        start=(a == 0 and t == 0),
                        stop=(a == 1 and t == PACK - 1),
                    )
        mag16 = work.tile([P, S, PACK], BF16, name="mag16", tag="first0", bufs=1, align_bytes=64)
        for c in range(4):
            nc.scalar.activation(
                mag16[:, c * P : (c + 1) * P, :], mag_banks[c][:].rearrange("p t n -> p n t"), ACT.Abs
            )
        mag_s = keep.tile([P, S], U8, name="mag_s", align_bytes=64)

        w_q, w_s = {}, {}

        def cast_w(b, g, half, stage, engine):
            dst = stage.rearrange("p t m j -> p m j t")
            src = w_raw[b, g][:].rearrange("p j (m t) -> p m j t", t=PACK)[:, :, :, 2 * half : 2 * half + 2]
            if engine == "vector":
                nc.vector.tensor_copy(dst, src)
            else:
                nc.scalar.copy(dst, src)

        def quant_w(b, g, t0, t1, stage, codes=None):
            width = (t1 - t0) * P
            if codes is None:
                codes = work.tile([P, width], U32, name=f"w_q{b}_{g}", tag="w_q", bufs=6, align_bytes=64)[:]
            if (b, g) not in w_s:
                w_s[b, g] = work.tile([P, KP], U8, name=f"w_s{b}_{g}", tag="w_s", bufs=6, align_bytes=64)
            for t in range(t0, t1):
                w_q[b, g, t] = codes[:, (t - t0) * P : (t - t0 + 1) * P]
            nc.vector.quantize_mx(
                codes.bitcast(FP8X4), w_s[b, g][:, t0 * P : t1 * P], stage.rearrange("p t m j -> p (t m j)")
            )

        def prepare_w(b, g):
            stage = work.tile([P, PACK, P, PACK], BF16, name=f"w16_{b}_{g}", tag="w16", bufs=3, align_bytes=64)
            for half in range(2):
                cast_w(b, g, half, stage[:, 2 * half : 2 * half + 2], "scalar")
            quant_w(b, g, 0, PACK, stage[:])

        for g in (1, 2, 0):
            stage = work.tile([P, 2, P, PACK], BF16, name=f"w16_first{g}", tag=f"first{g}", bufs=1, align_bytes=64)
            cast_w(0, g, 0, stage[:], "vector")
            quant_w(0, g, 0, 2, stage[:])
            if g == 2:
                mag_q = work.tile([P, S], U32, name="mag_q", tag="first2", bufs=1, align_bytes=64)
                nc.vector.quantize_mx(mag_q[:].bitcast(FP8X4), mag_s[:], mag16[:].rearrange("p n t -> p (n t)"))

        near_sb, deep_bank, hs, ds = {}, {}, {}, {}

        def products(s):
            b, t = divmod(s, PACK)
            cols = slice(t * P, (t + 1) * P)
            near = bank([P, S], f"near{s}")
            for a in range(2):
                nc.tensor.matmul_mx(
                    near[:], lhsT=w_q[b, 1 + a, t].bitcast(FP8X4), lhsT_scale=w_s[b, 1 + a][:, cols],
                    rhs=vw[a][:].bitcast(FP8X4), rhs_scale=vs[a][:], start=(a == 0), stop=(a == 1),
                )
            nsb = work.tile([P, S], F32, name=f"near_sb{s}", tag="near_sb", bufs=2)
            nc.scalar.copy(nsb[:], near[:])
            deep = bank([P, S], f"deep{s}")
            nc.tensor.matmul_mx(
                deep[:], lhsT=w_q[b, 0, t].bitcast(FP8X4), lhsT_scale=w_s[b, 0][:, cols],
                rhs=mag_q[:].bitcast(FP8X4), rhs_scale=mag_s[:], start=True, stop=True,
            )
            near_sb[s], deep_bank[s] = nsb, deep

        def larger(s):
            tag = "h_a" if s % 2 == 0 and s != 2 else "h_b"
            h = work.tile([P, S], F32, name=f"h{s}", tag=tag, bufs=1, align_bytes=64)
            nc.vector.tensor_tensor(h[:], deep_bank[s][:], near_sb[s][:], ALU.max)
            hs[s] = h

        def scatter(s):
            nc.vector.tensor_tensor(pages[s][:].indirect(o2[:]), hs[s][:], wg[s % PACK][:], ALU.mult)

        def gather(s, cols, minuend, dst):
            entries = o3[:, cols.start // 16 : cols.stop // 16]
            nc.vector.tensor_tensor(dst, pages[s][:].indirect(entries), minuend, ALU.subtract)
            ds[s] = dst

        x_planes, x16, x_q, x_s = {}, {}, {}, {}
        page_planes, page16, page_q, page_s = {}, {}, {}, {}

        def clamp(s, cols):
            b, t = divmod(s, PACK)
            if t == 0:
                x_planes[b] = work.tile([P, PACK, PJ], BF16, name=f"x_planes{b}", tag="x_planes")
            nc.vector.tensor_scalar(
                x_planes[b][:, t, cols], ds[s], neg_lim[:, s : s + 1], neg_gain[:, s : s + 1],
                ALU.min, ALU.mult,
            )

        def clamp_on_scalar(s):
            b, t = divmod(s, PACK)
            if t == 0:
                x_planes[b] = work.tile([P, PACK, PJ], BF16, name=f"x_planes{b}", tag="x_planes")
            above = work.tile([P, PJ], F32, name=f"above{s}", tag="above")
            nc.scalar.activation(above[:], ds[s], ACT.Relu, bias=neg_lim[:, s : s + 1], scale=-1.0)
            nc.scalar.activation(
                x_planes[b][:, t, :], above[:], ACT.Identity,
                bias=floor[:, s : s + 1], scale=gain_sb[:, b, t : t + 1],
            )

        def weave(dst, src, engine):
            dst = dst.rearrange("p (c i) t -> p c t i", i=4)
            src = src.rearrange("p t (c i) -> p c t i", i=4)
            if engine == "vector":
                nc.vector.tensor_copy(dst, src)
            else:
                nc.scalar.copy(dst, src)

        def weave_x(b, cols, engine):
            if cols.start == 0:
                x16[b] = work.tile([P, PJ, PACK], BF16, name=f"x16_{b}", tag="x16", bufs=2, align_bytes=64)
            weave(x16[b][:, cols, :], x_planes[b][:, :, cols], engine)

        def quant_x(b, cols):
            if cols.start == 0:
                x_q[b] = keep.tile([P, PJ], U32, name=f"x_q{b}", align_bytes=64)
                x_s[b] = keep.tile([P, PJ], U8, name=f"x_s{b}", align_bytes=64)
            nc.vector.quantize_mx(
                x_q[b][:, cols].bitcast(FP8X4), x_s[b][:, cols], x16[b][:, cols, :].rearrange("p n t -> p (n t)")
            )

        def cast_page(s):
            b, t = divmod(s, PACK)
            if t == 0:
                page_planes[b] = work.tile([P, PACK, T2], BF16, name=f"page_planes{b}", tag="page_planes")
            nc.scalar.copy(page_planes[b][:, t, :], pages[s][:])

        def weave_page(b):
            for u in range(2):
                page16[b, u] = work.tile([P, T2 // 2, PACK], BF16, name=f"page16_{b}_{u}", tag=(f"page16_{u}" if b == 2 or 1 == 0 else f"page16x_{u}"), bufs=1, align_bytes=64)
                for v in range(2):
                    lo = u * 512 + v * 256
                    weave(page16[b, u][:, v * 256 : (v + 1) * 256, :], page_planes[b][:, :, lo : lo + 256], "scalar")

        def quant_page(b, u):
            if u == 0:
                page_q[b] = keep.tile([P, T2], U32, name=f"page_q{b}", align_bytes=64)
                page_s[b] = keep.tile([P, T2], U8, name=f"page_s{b}", align_bytes=64)
            cols = slice(u * 512, (u + 1) * 512)
            nc.vector.quantize_mx(
                page_q[b][:, cols].bitcast(FP8X4), page_s[b][:, cols], page16[b, u][:].rearrange("p m t -> p (m t)")
            )

        halves = (slice(0, PJ // 2), slice(PJ // 2, PJ))
        whole = slice(0, PJ)
        e_banks = {}

        def score(half, k, b):
            if b == 0:
                e_banks[half, k] = bank([P, 2, PJ // 2], f"e{half}_{k}")
            for i in range(2):
                cols = slice((2 * k + i) * P, (2 * k + i + 1) * P)
                nc.tensor.matmul_mx(
                    e_banks[half, k][:, i, :], lhsT=page_q[b][:, cols].bitcast(FP8X4), lhsT_scale=page_s[b][:, cols],
                    rhs=x_q[b][:, halves[half]].bitcast(FP8X4), rhs_scale=x_s[b][:, halves[half]],
                    start=(b == 0 and i == 0), stop=(b == BLOCKS - 1 and i == 1),
                )

        products(0)
        first_h = []
        for half, tag in enumerate(("h_a", "h_b")):
            h = work.tile([P, S // 2], F32, name=f"h0_{half}", tag=tag, bufs=1, align_bytes=64)
            nc.vector.tensor_tensor(h[:], deep_bank[0][:, halves[half]], near_sb[0][:, halves[half]], ALU.max)
            first_h.append(h)
        for half in range(2):
            cols = halves[half]
            places = o2[:, cols.start // 16 : cols.stop // 16]
            nc.vector.tensor_tensor(pages[0][:].indirect(places), first_h[half][:], wg[0][:, cols], ALU.mult)
        late = work.tile([P, 3, 2, P, PACK], BF16, name="w16_second", tag="first0", bufs=1, align_bytes=64)
        late_q = work.tile([P, 3, 2 * P], U32, name="w_q_second", tag="h_a", bufs=1, align_bytes=64)
        for g in (1, 2, 0):
            cast_w(0, g, 1, late[:, g], "scalar")
            quant_w(0, g, 2, PACK, late[:, g], late_q[:, g, :])
            if g == 1:
                products(1)
                larger(1)

        last = SLICES - 1
        later_w = [(b, g) for b in range(1, BLOCKS) for g in (1, 2, 0)]
        wpos = [1, 2, 3, 4, 5, 6]
        for s in range(SLICES):
            b, t = divmod(s, PACK)
            nxt = s + 2
            if nxt < SLICES:
                if nxt < PACK:
                    load_wg(nxt)
                for i in range(1, 6):
                    if wpos[i] == nxt:
                        load_w(*later_w[i])
                load_page(nxt)
                if s == 0:
                    nc.sync.dma_start(lim_sb[:], lim.rearrange("(a p t) -> p a t", p=P, t=PACK))
                    nc.sync.dma_start(gain_sb[:], gain.rearrange("(a p t) -> p a t", p=P, t=PACK))
                    nc.sync.dma_start(o3[:], offs3)
                    nc.scalar.mul(neg_lim[:], lim_sb[:].rearrange("p a t -> p (a t)"), -1.0)
                    nc.scalar.mul(neg_gain[:], gain_sb[:].rearrange("p a t -> p (a t)"), -1.0)
                    nc.vector.tensor_tensor(floor[:], neg_lim[:], neg_gain[:], ALU.mult)
                if nxt < last:
                    load_base(s)
            if s == PACK + 2:
                with nc.allow_non_contiguous_dma(reason="one bias value a partition"):
                    nc.sync.dma_start(slot_sb[:], slot.rearrange("(c p) -> p c", p=P))
            if s > 0:
                scatter(s)
            if s == last - 1:
                tail_base = []
                for half in range(2):
                    bs = work.tile([P, 3, PJ // 2], F32, name=f"tail_base{half}", tag=f"wg{2 + half}", bufs=1)
                    src = base[(BLOCKS - 1) * KP :, halves[half]].rearrange("(p t) c -> p t c", t=PACK)
                    nc.sync.dma_start(bs[:], src[:, 1:PACK, :])
                    tail_base.append(bs)
            for i in range(6):
                if max(wpos[i] - 1, 0) == s:
                    prepare_w(*later_w[i])
                    if 0 and i % 3 == 2:
                        for r in range(4):
                            products(4 * later_w[i][0] + r)
            ready = [s + 1] if s < PACK else []
            if PACK - 1 <= s and nxt < SLICES:
                ready.append(nxt)
            if s == 0:
                ready = []
            for r in ready:
                if r not in near_sb:
                    products(r)
            cast_page(s)
            if 2 <= s < last:
                d = work.tile([P, PJ], F32, name=f"d{s - 2}", tag="d", bufs=2)
                gather(s - 2, whole, bases[s - 2][:], d[:])
            for r in ready:
                larger(r)
            if 2 <= s < last:
                if s - 2 < 9 and s - 2 >= 0:
                    clamp_on_scalar(s - 2)
                else:
                    clamp(s - 2, whole)
            if t == 1 and b > 0:
                weave_page(b - 1)
            if t == 2 and b > 0:
                quant_page(b - 1, 0)
                quant_page(b - 1, 1)
                for half in range(2):
                    weave_x(b - 1, halves[half], "scalar")
                quant_x(b - 1, whole)
            if s == last - 1:
                for half in range(2):
                    for k in range(CHUNKS // 2):
                        for bb in range(BLOCKS - 1):
                            score(half, k, bb)
        weave_page(BLOCKS - 1)
        b = BLOCKS - 1
        for half in range(2):
            cols = halves[half]
            if half == 0:
                d = work.tile([P, 3, PJ // 2], F32, name="d_tail0", tag="d", bufs=2)
                dsts = [d[:, i, :] for i in range(3)]
            else:
                if 0 == 0:
                    d = work.tile([P, PJ // 2], F32, name="d_tail1", tag="page16_0", bufs=1, align_bytes=64)
                    d_last = work.tile([P, 2, PJ // 2], F32, name="d_tail2", tag="page16_1", bufs=1, align_bytes=64)
                    dsts = [d[:], d_last[:, 0, :], d_last[:, 1, :]]
                else:
                    d0 = work.tile([P, PJ // 2], F32, name="d_tail1a", tag="d_free", bufs=1)
                    d = work.tile([P, PJ // 2], F32, name="d_tail1", tag="page16_0", bufs=1, align_bytes=64)
                    d_last = work.tile([P, PJ // 2], F32, name="d_tail2", tag="page16_1", bufs=1, align_bytes=64)
                    dsts = [d0[:], d[:], d_last[:]]
            for i, s in enumerate(range(last - 2, SLICES)):
                gather(s, cols, tail_base[half][:, i, :], dsts[i])
            for s in range(last - 2, SLICES):
                clamp(s, cols)
            weave_x(b, cols, "vector")
            if half == 0:
                quant_page(b, 0)
            quant_x(b, cols)
            if half == 0:
                quant_page(b, 1)
            res = big([P, CHUNKS, PJ // 2], F32, f"res{half}")
            for k in range(CHUNKS // 2):
                score(half, k, b)
                for i in range(2):
                    c = 2 * k + i
                    nc.scalar.activation(
                        res[:, c, :], e_banks[half, k][:, i, :], ACT.Sigmoid, bias=slot_sb[:, c : c + 1]
                    )
                nc.sync.dma_start(
                    out[2 * k * P : (2 * k + 2) * P, cols].rearrange("(i p) j -> p i j", p=P),
                    res[:, 2 * k : 2 * k + 2, :],
                )
